import numpy as np
CORES = [60,61,62,63,176,177,178]
N = 7
W, H, TIMES = 64, 3, 1
WTS = [1,1,2,3,2,1,1]
def setup_inputs(rng):
    return {"x": rng.standard_normal((N, 128, W), dtype=np.float32)}
def reference(x):
    g = np.concatenate(list(x.astype(np.float64)), axis=1)
    for _ in range(TIMES):
        p = np.concatenate([g[:, -H:], g, g[:, :H]], axis=1)
        g = sum(WTS[i] * p[:, i:i + N * W] for i in range(2 * H + 1))
    return {"y": np.stack([g[:, W * r:W * r + W] for r in range(N)]).astype(np.float32 if x.dtype != np.float64 else np.float64)}

@@ -1,0 +1,120 @@
+from concourse.bass import DstId, RemoteDMATransfer
+from concourse.mybir import AluOpType
+
+SCRATCH = {
+    "p": ("sbuf", [128, 72], "float32"),
+    "a2": ("sbuf", [128, 72], "float32"),
+    "q4": ("sbuf", [128, 72], "float32"),
+    "s3": ("sbuf", [128, 72], "float32"),
+    "t": ("sbuf", [128, 64], "float32"),
+    "yb": ("sbuf", [128, 64], "float32"),
+    "hl": ("sbuf", [128, 4], "float32"),
+    "hr": ("sbuf", [128, 4], "float32"),
+    "rec": ("dram", [128, 3], "float32"),
+    "rly": ("dram", [128, 3], "float32"),
+}
+SEMAPHORES = ["ld", "eld", "ms", "v", "al", "ar", "snt", "st1", "st2", "rl"]
+
+RELAY = {176: 50, 60: 190}
+
+
+def rank_program(g, core, T, topo):
+    S = T.sem
+    cores = list(T.cores)
+    n = len(cores)
+
+    for src, rel in RELAY.items():
+        if core == rel:
+            dst = cores[(T.rank_of(src) - 1) % n]
+            rid, pid = topo.addr(dst, core)
+            g.wait_ge(S.rl, 8)
+            g.remote_dma(T.hr[:, 0:3], T.rly[:], S.ar, S.snt, pid, rid, 0x00FF)
+            g.wait_ge(S.snt, 8)
+            return
+
+    rank = T.rank_of(core)
+    if rank is None:
+        return
+    left, right = cores[(rank - 1) % n], cores[(rank + 1) % n]
+    relayed = core in RELAY
+
+    if relayed:
+        g.sync.dma_start(T.rec[:], T.x[:, 0:3]).then_inc(S.eld, 16)
+    g.sync.dma_start(T.p[:, 4:68], T.x[:]).then_inc(S.ld, 16)
+
+    rr, rp = topo.addr(right, core)
+    if relayed:
+        rel = RELAY[core]
+        qr, qp = topo.addr(rel, core)
+        g.wait_ge(S.eld, 16)
+        g.remote_dma(T.rly[:], T.rec[:], S.rl, S.snt, qp, qr, 0x00FF)
+        g.wait_ge(S.ld, 16)
+        g.remote_dma(T.hl[:, 0:3], T.p[:, 65:68], S.al, S.snt, rp, rr, 0xFFFF)
+        sent = 24
+    else:
+        lr, lp = topo.addr(left, core)
+        off_right = topo.mask(core, right) == 0x00FF
+        m_right, m_left = (0x00FF, 0xFF00) if off_right else (0xFF00, 0x00FF)
+        g.wait_ge(S.ld, 16)
+        g.remote_dma_fused([
+            RemoteDMATransfer(dst_ids=[DstId(rid=lr, pnc=lp)], dma_engine_mask=m_left, remote_sem=S.ar,
+                              src=T.p[:, 4:7], dst=T.hr[:, 0:3]),
+            RemoteDMATransfer(dst_ids=[DstId(rid=rr, pnc=rp)], dma_engine_mask=m_right, remote_sem=S.al,
+                              src=T.p[:, 65:68], dst=T.hl[:, 0:3]),
+        ], local_sem=S.snt)
+        sent = 16
+    g.wait_ge(S.snt, sent)
+
+    v = g.vector
+    cnt = [0]
+
+    def add(out, a, b):
+        if cnt[0]:
+            v.wait_ge(S.v, cnt[0])
+        v.tensor_tensor(out, a, b, AluOpType.add).then_inc(S.v, 1)
+        cnt[0] += 1
+
+    v.memset(T.p[:, 0:4], 0.0).then_inc(S.ms, 1)
+    v.memset(T.p[:, 68:72], 0.0).then_inc(S.ms, 1)
+    v.wait_ge(S.ms, 2)
+    v.wait_ge(S.ld, 16)
+    add(T.a2[:, 1:70], T.p[:, 1:70], T.p[:, 2:71])
+    add(T.q4[:, 1:68], T.a2[:, 1:68], T.a2[:, 3:70])
+    add(T.s3[:, 3:67], T.a2[:, 3:67], T.p[:, 5:69])
+    add(T.t[:, 0:64], T.q4[:, 1:65], T.q4[:, 4:68])
+    add(T.yb[:, 0:64], T.t[:, 0:64], T.s3[:, 3:67])
+
+    def fix_left():
+        v.wait_ge(S.al, 16 if left in RELAY else 8)
+        add(T.yb[:, 0:3], T.yb[:, 0:3], T.hl[:, 0:3])
+        add(T.yb[:, 0:2], T.yb[:, 0:2], T.hl[:, 1:3])
+        add(T.yb[:, 0:1], T.yb[:, 0:1], T.hl[:, 2:3])
+        add(T.yb[:, 0:1], T.yb[:, 0:1], T.hl[:, 2:3])
+
+    def fix_right():
+        v.wait_ge(S.ar, 8)
+        add(T.yb[:, 61:64], T.yb[:, 61:64], T.hr[:, 0:3])
+        add(T.yb[:, 62:64], T.yb[:, 62:64], T.hr[:, 0:2])
+        add(T.yb[:, 63:64], T.yb[:, 63:64], T.hr[:, 0:1])
+        add(T.yb[:, 63:64], T.yb[:, 63:64], T.hr[:, 0:1])
+
+    left_last = topo.mask(left, core) != 0xFFFF and not topo.mask(core, left) == 0xFFFF
+    if left_last:
+        fix_right()
+        early, late = (4, 64), (0, 4)
+    else:
+        fix_left()
+        early, late = (0, 60), (60, 64)
+    n_early = cnt[0]
+    if left_last:
+        fix_left()
+    else:
+        fix_right()
+    n_all = cnt[0]
+
+    g.scalar.wait_ge(S.v, n_early)
+    g.scalar.dma_start(T.y[:, early[0]:early[1]], T.yb[:, early[0]:early[1]]).then_inc(S.st1, 16)
+    g.scalar.wait_ge(S.st1, 16)
+    g.sync.wait_ge(S.v, n_all)
+    g.sync.dma_start(T.y[:, late[0]:late[1]], T.yb[:, late[0]:late[1]]).then_inc(S.st2, 16)
+    g.sync.wait_ge(S.st2, 16)

@@ -3,13 +3,15 @@ from concourse.mybir import AluOpType
 
 SCRATCH = {
     "p": ("sbuf", [128, 72], "float32"),
-    "a2": ("sbuf", [128, 72], "float32"),
+    "a2": ("psum", [128, 72], "float32"),
+    "s3": ("psum", [128, 72], "float32"),
     "q4": ("sbuf", [128, 72], "float32"),
-    "s3": ("sbuf", [128, 72], "float32"),
     "t": ("sbuf", [128, 64], "float32"),
-    "yb": ("sbuf", [128, 64], "float32"),
+    "Y": ("sbuf", [128, 72], "float32"),
     "hl": ("sbuf", [128, 4], "float32"),
     "hr": ("sbuf", [128, 4], "float32"),
+    "u": ("sbuf", [128, 8], "float32"),
+    "w": ("sbuf", [128, 4], "float32"),
     "rec": ("dram", [128, 3], "float32"),
     "rly": ("dram", [128, 3], "float32"),
 }
@@ -23,12 +25,25 @@ def rank_program(g, core, T, topo):
     cores = list(T.cores)
     n = len(cores)
 
+    def left_of(c):
+        return cores[(T.rank_of(c) - 1) % n]
+
+    def left_late(c):
+        l = left_of(c)
+        return (topo.host(l), topo.chip(l)) != (topo.host(c), topo.chip(c)) or l in RELAY
+
+    def right_landing(c):
+        return T.hr[:, 0:3] if left_late(c) else T.Y[:, 68:71]
+
+    def left_landing(c):
+        return T.Y[:, 1:4] if left_late(c) else T.hl[:, 0:3]
+
     for src, rel in RELAY.items():
         if core == rel:
-            dst = cores[(T.rank_of(src) - 1) % n]
+            dst = left_of(src)
             rid, pid = topo.addr(dst, core)
             g.wait_ge(S.rl, 8)
-            g.remote_dma(T.hr[:, 0:3], T.rly[:], S.ar, S.snt, pid, rid, 0x00FF)
+            g.remote_dma(right_landing(dst), T.rly[:], S.ar, S.snt, pid, rid, 0x00FF)
             g.wait_ge(S.snt, 8)
             return
 
@@ -44,12 +59,11 @@ def rank_program(g, core, T, topo):
 
     rr, rp = topo.addr(right, core)
     if relayed:
-        rel = RELAY[core]
-        qr, qp = topo.addr(rel, core)
+        qr, qp = topo.addr(RELAY[core], core)
         g.wait_ge(S.eld, 16)
         g.remote_dma(T.rly[:], T.rec[:], S.rl, S.snt, qp, qr, 0x00FF)
         g.wait_ge(S.ld, 16)
-        g.remote_dma(T.hl[:, 0:3], T.p[:, 65:68], S.al, S.snt, rp, rr, 0xFFFF)
+        g.remote_dma(left_landing(right), T.p[:, 65:68], S.al, S.snt, rp, rr, 0xFFFF)
         sent = 24
     else:
         lr, lp = topo.addr(left, core)
@@ -58,9 +72,9 @@ def rank_program(g, core, T, topo):
         g.wait_ge(S.ld, 16)
         g.remote_dma_fused([
             RemoteDMATransfer(dst_ids=[DstId(rid=lr, pnc=lp)], dma_engine_mask=m_left, remote_sem=S.ar,
-                              src=T.p[:, 4:7], dst=T.hr[:, 0:3]),
+                              src=T.p[:, 4:7], dst=right_landing(left)),
             RemoteDMATransfer(dst_ids=[DstId(rid=rr, pnc=rp)], dma_engine_mask=m_right, remote_sem=S.al,
-                              src=T.p[:, 65:68], dst=T.hl[:, 0:3]),
+                              src=T.p[:, 65:68], dst=left_landing(right)),
         ], local_sem=S.snt)
         sent = 16
     g.wait_ge(S.snt, sent)
@@ -68,53 +82,60 @@ def rank_program(g, core, T, topo):
     v = g.vector
     cnt = [0]
 
-    def add(out, a, b):
+    def add(out, a, b, op=AluOpType.add):
         if cnt[0]:
             v.wait_ge(S.v, cnt[0])
-        v.tensor_tensor(out, a, b, AluOpType.add).then_inc(S.v, 1)
         cnt[0] += 1
+        v.tensor_tensor(out, a, b, op).then_inc(S.v, 1)
+
+    ll = left_late(core)
+    o = 5 if ll else 3
+    zc = 4 if ll else 67
+    n_al = 16 if left in RELAY else 8
+    Y, U, W = T.Y, T.u, T.w
 
     v.memset(T.p[:, 0:4], 0.0).then_inc(S.ms, 1)
     v.memset(T.p[:, 68:72], 0.0).then_inc(S.ms, 1)
-    v.wait_ge(S.ms, 2)
+    v.memset(Y[:, zc:zc + 1], 0.0).then_inc(S.ms, 1)
+    v.wait_ge(S.ms, 3)
     v.wait_ge(S.ld, 16)
     add(T.a2[:, 1:70], T.p[:, 1:70], T.p[:, 2:71])
-    add(T.q4[:, 1:68], T.a2[:, 1:68], T.a2[:, 3:70])
-    add(T.s3[:, 3:67], T.a2[:, 3:67], T.p[:, 5:69])
+    add(T.s3[:, 1:68], T.a2[:, 1:68], T.p[:, 3:70])
+    add(T.q4[:, 1:68], T.s3[:, 1:68], T.p[:, 4:71])
     add(T.t[:, 0:64], T.q4[:, 1:65], T.q4[:, 4:68])
-    add(T.yb[:, 0:64], T.t[:, 0:64], T.s3[:, 3:67])
+    add(Y[:, o:o + 64], T.t[:, 0:64], T.s3[:, 3:67])
 
-    def fix_left():
-        v.wait_ge(S.al, 16 if left in RELAY else 8)
-        add(T.yb[:, 0:3], T.yb[:, 0:3], T.hl[:, 0:3])
-        add(T.yb[:, 0:2], T.yb[:, 0:2], T.hl[:, 1:3])
-        add(T.yb[:, 0:1], T.yb[:, 0:1], T.hl[:, 2:3])
-        add(T.yb[:, 0:1], T.yb[:, 0:1], T.hl[:, 2:3])
-
-    def fix_right():
+    if ll:
+        add(U[:, 3:5], Y[:, 6:8], Y[:, 4:6], AluOpType.subtract)
         v.wait_ge(S.ar, 8)
-        add(T.yb[:, 61:64], T.yb[:, 61:64], T.hr[:, 0:3])
-        add(T.yb[:, 62:64], T.yb[:, 62:64], T.hr[:, 0:2])
-        add(T.yb[:, 63:64], T.yb[:, 63:64], T.hr[:, 0:1])
-        add(T.yb[:, 63:64], T.yb[:, 63:64], T.hr[:, 0:1])
-
-    left_last = topo.mask(left, core) != 0xFFFF and not topo.mask(core, left) == 0xFFFF
-    if left_last:
-        fix_right()
+        add(Y[:, o + 61:o + 64], Y[:, o + 61:o + 64], T.hr[:, 0:3])
+        add(Y[:, o + 62:o + 64], Y[:, o + 62:o + 64], T.hr[:, 0:2])
+        add(Y[:, o + 63:o + 64], Y[:, o + 63:o + 64], T.hr[:, 0:1])
+        add(Y[:, o + 63:o + 64], Y[:, o + 63:o + 64], T.hr[:, 0:1])
+        n_early = cnt[0]
         early, late = (4, 64), (0, 4)
+        v.wait_ge(S.al, n_al)
+        add(U[:, 0:3], Y[:, 1:4], Y[:, 3:6])
+        add(W[:, 0:3], U[:, 0:3], U[:, 2:5])
+        add(Y[:, 5:8], W[:, 0:3], Y[:, 2:5])
     else:
-        fix_left()
+        add(U[:, 0:2], Y[:, 64:66], Y[:, 66:68], AluOpType.subtract)
+        v.wait_ge(S.al, n_al)
+        add(Y[:, o:o + 3], Y[:, o:o + 3], T.hl[:, 0:3])
+        add(Y[:, o:o + 2], Y[:, o:o + 2], T.hl[:, 1:3])
+        add(Y[:, o:o + 1], Y[:, o:o + 1], T.hl[:, 2:3])
+        add(Y[:, o:o + 1], Y[:, o:o + 1], T.hl[:, 2:3])
+        n_early = cnt[0]
         early, late = (0, 60), (60, 64)
-    n_early = cnt[0]
-    if left_last:
-        fix_left()
-    else:
-        fix_right()
+        v.wait_ge(S.ar, 8)
+        add(U[:, 2:5], Y[:, 66:69], Y[:, 68:71])
+        add(W[:, 0:3], U[:, 0:3], U[:, 2:5])
+        add(Y[:, 64:67], W[:, 0:3], Y[:, 67:70])
     n_all = cnt[0]
 
     g.scalar.wait_ge(S.v, n_early)
-    g.scalar.dma_start(T.y[:, early[0]:early[1]], T.yb[:, early[0]:early[1]]).then_inc(S.st1, 16)
+    g.scalar.dma_start(T.y[:, early[0]:early[1]], Y[:, o + early[0]:o + early[1]]).then_inc(S.st1, 16)
     g.scalar.wait_ge(S.st1, 16)
     g.sync.wait_ge(S.v, n_all)
-    g.sync.dma_start(T.y[:, late[0]:late[1]], T.yb[:, late[0]:late[1]]).then_inc(S.st2, 16)
+    g.sync.dma_start(T.y[:, late[0]:late[1]], Y[:, o + late[0]:o + late[1]]).then_inc(S.st2, 16)
     g.sync.wait_ge(S.st2, 16)

@@ -3,8 +3,8 @@ from concourse.mybir import AluOpType
 
 SCRATCH = {
     "p": ("sbuf", [128, 72], "float32"),
-    "a2": ("psum", [128, 72], "float32"),
-    "s3": ("psum", [128, 72], "float32"),
+    "a2": ("sbuf", [128, 72], "float32"),
+    "s3": ("sbuf", [128, 72], "float32"),
     "q4": ("sbuf", [128, 72], "float32"),
     "t": ("sbuf", [128, 64], "float32"),
     "Y": ("sbuf", [128, 72], "float32"),
@@ -25,25 +25,12 @@ def rank_program(g, core, T, topo):
     cores = list(T.cores)
     n = len(cores)
 
-    def left_of(c):
-        return cores[(T.rank_of(c) - 1) % n]
-
-    def left_late(c):
-        l = left_of(c)
-        return (topo.host(l), topo.chip(l)) != (topo.host(c), topo.chip(c)) or l in RELAY
-
-    def right_landing(c):
-        return T.hr[:, 0:3] if left_late(c) else T.Y[:, 68:71]
-
-    def left_landing(c):
-        return T.Y[:, 1:4] if left_late(c) else T.hl[:, 0:3]
-
     for src, rel in RELAY.items():
         if core == rel:
-            dst = left_of(src)
+            dst = cores[(T.rank_of(src) - 1) % n]
             rid, pid = topo.addr(dst, core)
             g.wait_ge(S.rl, 8)
-            g.remote_dma(right_landing(dst), T.rly[:], S.ar, S.snt, pid, rid, 0x00FF)
+            g.remote_dma(T.Y[:, 68:71], T.rly[:], S.ar, S.snt, pid, rid, 0x00FF)
             g.wait_ge(S.snt, 8)
             return
 
@@ -52,30 +39,38 @@ def rank_program(g, core, T, topo):
         return
     left, right = cores[(rank - 1) % n], cores[(rank + 1) % n]
     relayed = core in RELAY
+    raw_right = right in RELAY
 
     if relayed:
         g.sync.dma_start(T.rec[:], T.x[:, 0:3]).then_inc(S.eld, 16)
     g.sync.dma_start(T.p[:, 4:68], T.x[:]).then_inc(S.ld, 16)
 
-    rr, rp = topo.addr(right, core)
+    p = T.p
+
+    def to_right(mask):
+        rr, rp = topo.addr(right, core)
+        return RemoteDMATransfer(dst_ids=[DstId(rid=rr, pnc=rp)], dma_engine_mask=mask, remote_sem=S.al, alu_op=1,
+                                 srcs=[p[:, 65:68], p[:, 66:69], p[:, 67:70], p[:, 67:70]], dsts=[T.hl[:, 0:3]])
+
+    def to_left(mask):
+        lr, lp = topo.addr(left, core)
+        return RemoteDMATransfer(dst_ids=[DstId(rid=lr, pnc=lp)], dma_engine_mask=mask, remote_sem=S.ar, alu_op=1,
+                                 srcs=[p[:, 4:7], p[:, 3:6], p[:, 2:5], p[:, 2:5]], dsts=[T.hr[:, 0:3]])
+
     if relayed:
         qr, qp = topo.addr(RELAY[core], core)
         g.wait_ge(S.eld, 16)
         g.remote_dma(T.rly[:], T.rec[:], S.rl, S.snt, qp, qr, 0x00FF)
+        g.wait_ge(S.ms, 3)
         g.wait_ge(S.ld, 16)
-        g.remote_dma(left_landing(right), T.p[:, 65:68], S.al, S.snt, rp, rr, 0xFFFF)
+        g.remote_dma_fused([to_right(0xFFFF)], local_sem=S.snt)
         sent = 24
     else:
-        lr, lp = topo.addr(left, core)
         off_right = topo.mask(core, right) == 0x00FF
         m_right, m_left = (0x00FF, 0xFF00) if off_right else (0xFF00, 0x00FF)
+        g.wait_ge(S.ms, 3)
         g.wait_ge(S.ld, 16)
-        g.remote_dma_fused([
-            RemoteDMATransfer(dst_ids=[DstId(rid=lr, pnc=lp)], dma_engine_mask=m_left, remote_sem=S.ar,
-                              src=T.p[:, 4:7], dst=right_landing(left)),
-            RemoteDMATransfer(dst_ids=[DstId(rid=rr, pnc=rp)], dma_engine_mask=m_right, remote_sem=S.al,
-                              src=T.p[:, 65:68], dst=left_landing(right)),
-        ], local_sem=S.snt)
+        g.remote_dma_fused([to_left(m_left), to_right(m_right)], local_sem=S.snt)
         sent = 16
     g.wait_ge(S.snt, sent)
 
@@ -88,50 +83,48 @@ def rank_program(g, core, T, topo):
         cnt[0] += 1
         v.tensor_tensor(out, a, b, op).then_inc(S.v, 1)
 
-    ll = left_late(core)
-    o = 5 if ll else 3
-    zc = 4 if ll else 67
+    o = 3
     n_al = 16 if left in RELAY else 8
     Y, U, W = T.Y, T.u, T.w
+    left_late = (topo.host(left), topo.chip(left)) != (topo.host(core), topo.chip(core)) or left in RELAY
 
-    v.memset(T.p[:, 0:4], 0.0).then_inc(S.ms, 1)
-    v.memset(T.p[:, 68:72], 0.0).then_inc(S.ms, 1)
-    v.memset(Y[:, zc:zc + 1], 0.0).then_inc(S.ms, 1)
+    v.memset(p[:, 0:4], 0.0).then_inc(S.ms, 1)
+    v.memset(p[:, 68:72], 0.0).then_inc(S.ms, 1)
+    v.memset(Y[:, 67:68], 0.0).then_inc(S.ms, 1)
     v.wait_ge(S.ms, 3)
     v.wait_ge(S.ld, 16)
-    add(T.a2[:, 1:70], T.p[:, 1:70], T.p[:, 2:71])
-    add(T.s3[:, 1:68], T.a2[:, 1:68], T.p[:, 3:70])
-    add(T.q4[:, 1:68], T.s3[:, 1:68], T.p[:, 4:71])
+    add(T.a2[:, 1:70], p[:, 1:70], p[:, 2:71])
+    add(T.s3[:, 1:68], T.a2[:, 1:68], p[:, 3:70])
+    add(T.q4[:, 1:68], T.s3[:, 1:68], p[:, 4:71])
     add(T.t[:, 0:64], T.q4[:, 1:65], T.q4[:, 4:68])
     add(Y[:, o:o + 64], T.t[:, 0:64], T.s3[:, 3:67])
 
-    if ll:
-        add(U[:, 3:5], Y[:, 6:8], Y[:, 4:6], AluOpType.subtract)
-        v.wait_ge(S.ar, 8)
-        add(Y[:, o + 61:o + 64], Y[:, o + 61:o + 64], T.hr[:, 0:3])
-        add(Y[:, o + 62:o + 64], Y[:, o + 62:o + 64], T.hr[:, 0:2])
-        add(Y[:, o + 63:o + 64], Y[:, o + 63:o + 64], T.hr[:, 0:1])
-        add(Y[:, o + 63:o + 64], Y[:, o + 63:o + 64], T.hr[:, 0:1])
-        n_early = cnt[0]
-        early, late = (4, 64), (0, 4)
-        v.wait_ge(S.al, n_al)
-        add(U[:, 0:3], Y[:, 1:4], Y[:, 3:6])
-        add(W[:, 0:3], U[:, 0:3], U[:, 2:5])
-        add(Y[:, 5:8], W[:, 0:3], Y[:, 2:5])
-    else:
-        add(U[:, 0:2], Y[:, 64:66], Y[:, 66:68], AluOpType.subtract)
+    def fix_left():
         v.wait_ge(S.al, n_al)
         add(Y[:, o:o + 3], Y[:, o:o + 3], T.hl[:, 0:3])
-        add(Y[:, o:o + 2], Y[:, o:o + 2], T.hl[:, 1:3])
-        add(Y[:, o:o + 1], Y[:, o:o + 1], T.hl[:, 2:3])
-        add(Y[:, o:o + 1], Y[:, o:o + 1], T.hl[:, 2:3])
+
+    def fix_right():
+        v.wait_ge(S.ar, 8)
+        add(Y[:, o + 61:o + 64], Y[:, o + 61:o + 64], T.hr[:, 0:3])
+
+    if raw_right:
+        add(U[:, 0:2], Y[:, 64:66], Y[:, 66:68], AluOpType.subtract)
+        fix_left()
         n_early = cnt[0]
-        early, late = (0, 60), (60, 64)
         v.wait_ge(S.ar, 8)
         add(U[:, 2:5], Y[:, 66:69], Y[:, 68:71])
         add(W[:, 0:3], U[:, 0:3], U[:, 2:5])
         add(Y[:, 64:67], W[:, 0:3], Y[:, 67:70])
+    elif left_late:
+        fix_right()
+        n_early = cnt[0]
+        fix_left()
+    else:
+        fix_left()
+        n_early = cnt[0]
+        fix_right()
     n_all = cnt[0]
+    early, late = ((4, 64), (0, 4)) if left_late else ((0, 60), (60, 64))
 
     g.scalar.wait_ge(S.v, n_early)
     g.scalar.dma_start(T.y[:, early[0]:early[1]], Y[:, o + early[0]:o + early[1]]).then_inc(S.st1, 16)

@@ -7,17 +7,18 @@ SCRATCH = {
     "s3": ("sbuf", [128, 72], "float32"),
     "q4": ("sbuf", [128, 72], "float32"),
     "t": ("sbuf", [128, 64], "float32"),
-    "Y": ("sbuf", [128, 72], "float32"),
+    "Y": ("sbuf", [128, 68], "float32"),
     "hl": ("sbuf", [128, 4], "float32"),
     "hr": ("sbuf", [128, 4], "float32"),
-    "u": ("sbuf", [128, 8], "float32"),
-    "w": ("sbuf", [128, 4], "float32"),
+    "Z": ("sbuf", [128, 2, 10], "float32"),
+    "G": ("sbuf", [128, 2, 4], "float32"),
     "rec": ("dram", [128, 3], "float32"),
     "rly": ("dram", [128, 3], "float32"),
 }
-SEMAPHORES = ["ld", "eld", "ms", "v", "al", "ar", "snt", "st1", "st2", "rl"]
+SEMAPHORES = ["ld", "eld", "ms", "al", "ar", "snt", "st0", "st1", "st2", "rl",
+              "k1", "k2", "k3", "k4", "k5", "kp", "kq", "ke", "i1", "kl"]
 
-RELAY = {176: 50, 60: 190}
+RELAY = {176: (50, 51), 60: (190, 191)}
 
 
 def rank_program(g, core, T, topo):
@@ -25,12 +26,13 @@ def rank_program(g, core, T, topo):
     cores = list(T.cores)
     n = len(cores)
 
-    for src, rel in RELAY.items():
-        if core == rel:
+    for src, rels in RELAY.items():
+        if core in rels:
             dst = cores[(T.rank_of(src) - 1) % n]
             rid, pid = topo.addr(dst, core)
-            g.wait_ge(S.rl, 8)
-            g.remote_dma(T.Y[:, 68:71], T.rly[:], S.ar, S.snt, pid, rid, 0x00FF)
+            landing = T.Z[:, 0, 4:7] if core == rels[0] else T.Z[:, 1, 6:9]
+            g.wait_ge(S.rl, 4)
+            g.remote_dma(landing, T.rly[:], S.ar, S.snt, pid, rid, 0x00FF)
             g.wait_ge(S.snt, 8)
             return
 
@@ -45,90 +47,93 @@ def rank_program(g, core, T, topo):
         g.sync.dma_start(T.rec[:], T.x[:, 0:3]).then_inc(S.eld, 16)
     g.sync.dma_start(T.p[:, 4:68], T.x[:]).then_inc(S.ld, 16)
 
-    p = T.p
+    p, s3 = T.p, T.s3
 
     def to_right(mask):
         rr, rp = topo.addr(right, core)
         return RemoteDMATransfer(dst_ids=[DstId(rid=rr, pnc=rp)], dma_engine_mask=mask, remote_sem=S.al, alu_op=1,
-                                 srcs=[p[:, 65:68], p[:, 66:69], p[:, 67:70], p[:, 67:70]], dsts=[T.hl[:, 0:3]])
+                                 srcs=[s3[:, 65:68], p[:, 67:70]], dsts=[T.hl[:, 0:3]])
 
     def to_left(mask):
         lr, lp = topo.addr(left, core)
         return RemoteDMATransfer(dst_ids=[DstId(rid=lr, pnc=lp)], dma_engine_mask=mask, remote_sem=S.ar, alu_op=1,
-                                 srcs=[p[:, 4:7], p[:, 3:6], p[:, 2:5], p[:, 2:5]], dsts=[T.hr[:, 0:3]])
+                                 srcs=[s3[:, 2:5], p[:, 2:5]], dsts=[T.hr[:, 0:3]])
 
     if relayed:
-        qr, qp = topo.addr(RELAY[core], core)
+        ar_, ap_ = topo.addr(RELAY[core][0], core)
+        br_, bp_ = topo.addr(RELAY[core][1], core)
         g.wait_ge(S.eld, 16)
-        g.remote_dma(T.rly[:], T.rec[:], S.rl, S.snt, qp, qr, 0x00FF)
-        g.wait_ge(S.ms, 3)
-        g.wait_ge(S.ld, 16)
+        g.remote_dma_fused([
+            RemoteDMATransfer(dst_ids=[DstId(rid=ar_, pnc=ap_)], dma_engine_mask=0x000F, remote_sem=S.rl,
+                              src=T.rec[:], dst=T.rly[:]),
+            RemoteDMATransfer(dst_ids=[DstId(rid=br_, pnc=bp_)], dma_engine_mask=0x00F0, remote_sem=S.rl, alu_op=1,
+                              srcs=[T.rec[:], T.rec[:]], dsts=[T.rly[:]]),
+        ], local_sem=S.snt)
+        g.wait_ge(S.k3, 1)
         g.remote_dma_fused([to_right(0xFFFF)], local_sem=S.snt)
         sent = 24
     else:
         off_right = topo.mask(core, right) == 0x00FF
         m_right, m_left = (0x00FF, 0xFF00) if off_right else (0xFF00, 0x00FF)
-        g.wait_ge(S.ms, 3)
-        g.wait_ge(S.ld, 16)
+        g.wait_ge(S.k3, 1)
         g.remote_dma_fused([to_left(m_left), to_right(m_right)], local_sem=S.snt)
         sent = 16
     g.wait_ge(S.snt, sent)
 
     v = g.vector
-    cnt = [0]
 
-    def add(out, a, b, op=AluOpType.add):
-        if cnt[0]:
-            v.wait_ge(S.v, cnt[0])
-        cnt[0] += 1
-        v.tensor_tensor(out, a, b, op).then_inc(S.v, 1)
+    def add(sem, needs, out, a, b, op=AluOpType.add):
+        for k in needs:
+            v.wait_ge(S[k], 1)
+        v.tensor_tensor(out, a, b, op).then_inc(S[sem], 1)
 
     o = 3
     n_al = 16 if left in RELAY else 8
-    Y, U, W = T.Y, T.u, T.w
+    Y, Z, G = T.Y, T.Z, T.G
     left_late = (topo.host(left), topo.chip(left)) != (topo.host(core), topo.chip(core)) or left in RELAY
 
     v.memset(p[:, 0:4], 0.0).then_inc(S.ms, 1)
     v.memset(p[:, 68:72], 0.0).then_inc(S.ms, 1)
     v.memset(Y[:, 67:68], 0.0).then_inc(S.ms, 1)
-    v.wait_ge(S.ms, 3)
+    v.memset(Z[:, 1, 3:4], 0.0).then_inc(S.ms, 1)
+    v.wait_ge(S.ms, 4)
     v.wait_ge(S.ld, 16)
-    add(T.a2[:, 1:70], p[:, 1:70], p[:, 2:71])
-    add(T.s3[:, 1:68], T.a2[:, 1:68], p[:, 3:70])
-    add(T.q4[:, 1:68], T.s3[:, 1:68], p[:, 4:71])
-    add(T.t[:, 0:64], T.q4[:, 1:65], T.q4[:, 4:68])
-    add(Y[:, o:o + 64], T.t[:, 0:64], T.s3[:, 3:67])
+    add("k1", [], T.a2[:, 1:70], p[:, 1:70], p[:, 2:71])
+    add("k3", ["k1"], s3[:, 1:70], T.a2[:, 1:70], p[:, 3:72])
+    add("k2", [], T.q4[:, 1:68], T.a2[:, 1:68], T.a2[:, 3:70])
+    add("k4", ["k2"], T.t[:, 0:64], T.q4[:, 1:65], T.q4[:, 4:68])
+    add("k5", ["k3", "k4"], Y[:, o:o + 64], T.t[:, 0:64], s3[:, 3:67])
+    v.wait_ge(S.k5, 1)
 
-    def fix_left():
+    def fix_left(sem):
         v.wait_ge(S.al, n_al)
-        add(Y[:, o:o + 3], Y[:, o:o + 3], T.hl[:, 0:3])
+        add(sem, [], Y[:, o:o + 3], Y[:, o:o + 3], T.hl[:, 0:3])
 
-    def fix_right():
+    def fix_right(sem):
         v.wait_ge(S.ar, 8)
-        add(Y[:, o + 61:o + 64], Y[:, o + 61:o + 64], T.hr[:, 0:3])
+        add(sem, [], Y[:, o + 61:o + 64], Y[:, o + 61:o + 64], T.hr[:, 0:3])
 
     if raw_right:
-        add(U[:, 0:2], Y[:, 64:66], Y[:, 66:68], AluOpType.subtract)
-        fix_left()
-        n_early = cnt[0]
-        v.wait_ge(S.ar, 8)
-        add(U[:, 2:5], Y[:, 66:69], Y[:, 68:71])
-        add(W[:, 0:3], U[:, 0:3], U[:, 2:5])
-        add(Y[:, 64:67], W[:, 0:3], Y[:, 67:70])
+        add("kp", [], Z[:, 1, 4:6], Y[:, 65:67], Y[:, 66:68], AluOpType.subtract)
+        add("kq", ["kp"], Z[:, 0, 3:4], Y[:, 64:65], Z[:, 1, 4:5], AluOpType.subtract)
+        fix_left("ke")
+        v.wait_ge(S.ar, 16)
+        add("i1", ["kq"], G[:, 0:2, 0:3], Z[:, 0:2, 3:6], Z[:, 0:2, 4:7])
+        add("kl", ["i1"], Y[:, 64:67], G[:, 0, 0:3], G[:, 1, 0:3])
     elif left_late:
-        fix_right()
-        n_early = cnt[0]
-        fix_left()
+        fix_right("ke")
+        fix_left("kl")
     else:
-        fix_left()
-        n_early = cnt[0]
-        fix_right()
-    n_all = cnt[0]
-    early, late = ((4, 64), (0, 4)) if left_late else ((0, 60), (60, 64))
+        fix_left("ke")
+        fix_right("kl")
+    early, late = ((60, 64), (0, 4)) if left_late else ((0, 4), (60, 64))
 
-    g.scalar.wait_ge(S.v, n_early)
+    g.scalar.wait_ge(S.k5, 1)
+    g.scalar.dma_start(T.y[:, 4:60], Y[:, o + 4:o + 60]).then_inc(S.st0, 16)
+    g.scalar.wait_ge(S.ke, 1)
     g.scalar.dma_start(T.y[:, early[0]:early[1]], Y[:, o + early[0]:o + early[1]]).then_inc(S.st1, 16)
+    g.scalar.wait_ge(S.st0, 16)
     g.scalar.wait_ge(S.st1, 16)
-    g.sync.wait_ge(S.v, n_all)
+    g.sync.wait_ge(S.kl, 1)
     g.sync.dma_start(T.y[:, late[0]:late[1]], Y[:, o + late[0]:o + late[1]]).then_inc(S.st2, 16)
     g.sync.wait_ge(S.st2, 16)

from concourse.bass import DstId, RemoteDMATransfer
from concourse.mybir import AluOpType

SCRATCH = {
    "p": ("sbuf", [128, 72], "float32"),
    "a2": ("sbuf", [128, 72], "float32"),
    "s3": ("sbuf", [128, 72], "float32"),
    "q4": ("sbuf", [128, 72], "float32"),
    "t": ("sbuf", [128, 64], "float32"),
    "Y": ("sbuf", [128, 68], "float32"),
    "hl": ("sbuf", [128, 4], "float32"),
    "hr": ("sbuf", [128, 4], "float32"),
    "Z": ("sbuf", [128, 2, 10], "float32"),
    "G": ("sbuf", [128, 2, 4], "float32"),
    "rec": ("dram", [128, 3], "float32"),
    "rly": ("dram", [128, 3], "float32"),
}
SEMAPHORES = ["ld", "eld", "ms", "al", "ar", "snt", "st0", "st1", "st2", "rl",
              "k1", "k2", "k3", "k4", "k5", "kp", "kq", "ke", "i1", "kl"]

RELAY = {176: (50, 51), 60: (190, 191)}


def rank_program(g, core, T, topo):
    S = T.sem
    cores = list(T.cores)
    n = len(cores)

    for src, rels in RELAY.items():
        if core in rels:
            dst = cores[(T.rank_of(src) - 1) % n]
            rid, pid = topo.addr(dst, core)
            landing = T.Z[:, 0, 4:7] if core == rels[0] else T.Z[:, 1, 6:9]
            g.wait_ge(S.rl, 4)
            g.remote_dma(landing, T.rly[:], S.ar, S.snt, pid, rid, 0x00FF)
            g.wait_ge(S.snt, 8)
            return

    rank = T.rank_of(core)
    if rank is None:
        return
    left, right = cores[(rank - 1) % n], cores[(rank + 1) % n]
    relayed = core in RELAY
    raw_right = right in RELAY

    if relayed:
        g.sync.dma_start(T.rec[:], T.x[:, 0:3]).then_inc(S.eld, 16)
    g.sync.dma_start(T.p[:, 4:68], T.x[:]).then_inc(S.ld, 16)

    p, s3 = T.p, T.s3

    def to_right(mask):
        rr, rp = topo.addr(right, core)
        return RemoteDMATransfer(dst_ids=[DstId(rid=rr, pnc=rp)], dma_engine_mask=mask, remote_sem=S.al, alu_op=1,
                                 srcs=[s3[:, 65:68], p[:, 67:70]], dsts=[T.hl[:, 0:3]])

    def to_left(mask):
        lr, lp = topo.addr(left, core)
        return RemoteDMATransfer(dst_ids=[DstId(rid=lr, pnc=lp)], dma_engine_mask=mask, remote_sem=S.ar, alu_op=1,
                                 srcs=[s3[:, 2:5], p[:, 2:5]], dsts=[T.hr[:, 0:3]])

    if relayed:
        ar_, ap_ = topo.addr(RELAY[core][0], core)
        br_, bp_ = topo.addr(RELAY[core][1], core)
        g.wait_ge(S.eld, 16)
        g.remote_dma_fused([
            RemoteDMATransfer(dst_ids=[DstId(rid=ar_, pnc=ap_)], dma_engine_mask=0x000F, remote_sem=S.rl,
                              src=T.rec[:], dst=T.rly[:]),
            RemoteDMATransfer(dst_ids=[DstId(rid=br_, pnc=bp_)], dma_engine_mask=0x00F0, remote_sem=S.rl, alu_op=1,
                              srcs=[T.rec[:], T.rec[:]], dsts=[T.rly[:]]),
        ], local_sem=S.snt)
        g.wait_ge(S.k3, 1)
        g.remote_dma_fused([to_right(0xFFFF)], local_sem=S.snt)
        sent = 24
    else:
        off_right = topo.mask(core, right) == 0x00FF
        m_right, m_left = (0x00FF, 0xFF00) if off_right else (0xFF00, 0x00FF)
        g.wait_ge(S.k3, 1)
        g.remote_dma_fused([to_left(m_left), to_right(m_right)], local_sem=S.snt)
        sent = 16
    g.wait_ge(S.snt, sent)

    v = g.vector

    def add(sem, needs, out, a, b, op=AluOpType.add):
        for k in needs:
            v.wait_ge(S[k], 1)
        v.tensor_tensor(out, a, b, op).then_inc(S[sem], 1)

    o = 3
    n_al = 16 if left in RELAY else 8
    Y, Z, G = T.Y, T.Z, T.G
    left_late = (topo.host(left), topo.chip(left)) != (topo.host(core), topo.chip(core)) or left in RELAY

    v.memset(p[:, 0:4], 0.0).then_inc(S.ms, 1)
    v.memset(p[:, 68:72], 0.0).then_inc(S.ms, 1)
    v.memset(Y[:, 67:68], 0.0).then_inc(S.ms, 1)
    v.memset(Z[:, 1, 3:4], 0.0).then_inc(S.ms, 1)
    v.wait_ge(S.ms, 4)
    v.wait_ge(S.ld, 16)
    add("k1", [], T.a2[:, 1:70], p[:, 1:70], p[:, 2:71])
    add("k3", ["k1"], s3[:, 1:70], T.a2[:, 1:70], p[:, 3:72])
    add("k2", [], T.q4[:, 1:68], T.a2[:, 1:68], T.a2[:, 3:70])
    add("k4", ["k2"], T.t[:, 0:64], T.q4[:, 1:65], T.q4[:, 4:68])
    add("k5", ["k3", "k4"], Y[:, o:o + 64], T.t[:, 0:64], s3[:, 3:67])
    v.wait_ge(S.k5, 1)

    def fix_left(sem):
        v.wait_ge(S.al, n_al)
        add(sem, [], Y[:, o:o + 3], Y[:, o:o + 3], T.hl[:, 0:3])

    def fix_right(sem):
        v.wait_ge(S.ar, 8)
        add(sem, [], Y[:, o + 61:o + 64], Y[:, o + 61:o + 64], T.hr[:, 0:3])

    if raw_right:
        add("kp", [], Z[:, 1, 4:6], Y[:, 65:67], Y[:, 66:68], AluOpType.subtract)
        add("kq", ["kp"], Z[:, 0, 3:4], Y[:, 64:65], Z[:, 1, 4:5], AluOpType.subtract)
        fix_left("ke")
        v.wait_ge(S.ar, 16)
        add("i1", ["kq"], G[:, 0:2, 0:3], Z[:, 0:2, 3:6], Z[:, 0:2, 4:7])
        add("kl", ["i1"], Y[:, 64:67], G[:, 0, 0:3], G[:, 1, 0:3])
    elif left_late:
        fix_right("ke")
        fix_left("kl")
    else:
        fix_left("ke")
        fix_right("kl")
    early, late = ((60, 64), (0, 4)) if left_late else ((0, 4), (60, 64))

    g.scalar.wait_ge(S.k5, 1)
    g.scalar.dma_start(T.y[:, 4:60], Y[:, o + 4:o + 60]).then_inc(S.st0, 16)
    g.scalar.wait_ge(S.ke, 1)
    g.scalar.dma_start(T.y[:, early[0]:early[1]], Y[:, o + early[0]:o + early[1]]).then_inc(S.st1, 16)
    g.scalar.wait_ge(S.st0, 16)
    g.scalar.wait_ge(S.st1, 16)
    g.sync.wait_ge(S.kl, 1)
    g.sync.dma_start(T.y[:, late[0]:late[1]], Y[:, o + late[0]:o + late[1]]).then_inc(S.st2, 16)
    g.sync.wait_ge(S.st2, 16)
